import numpy as np
import ml_dtypes


def mxq(x, axis, fmt="e4m3"):
    dtype, down = {"e4m3": (ml_dtypes.float8_e4m3fn, 7), "e5m2": (ml_dtypes.float8_e5m2, 14)}[fmt]
    v = np.moveaxis(np.asarray(x, np.float32).astype(ml_dtypes.bfloat16).astype(np.float64), axis, -1)
    blocks = v.reshape(v.shape[:-1] + (-1, 32))
    amax = np.abs(blocks).max(-1, keepdims=True)
    byte = np.maximum(np.where(amax > 0, np.frexp(amax)[1] - 1 + 127, 0) - down, 1)
    scale = np.exp2(byte - 127.0)
    codes = (blocks / scale).astype(np.float32).astype(dtype).astype(np.float64)
    return np.moveaxis((codes * scale).reshape(v.shape), -1, axis)


WIDE = False


def mx_kscale(k):
    if not WIDE:
        return np.ones(k)
    levels = np.array([10, -10, 5, -5, 0])
    if k % 512:
        return np.exp2(np.random.permutation(np.resize(levels, k // 32))).repeat(32)
    a = np.empty((k // 512, 16))
    for p in range(k // 512):
        a[p, :8] = np.random.permutation(np.resize(levels, 8))
        for g in range(8):
            far = levels[np.abs(levels - a[p, g]) >= 10]
            a[p, g + 8] = far[np.random.randint(len(far))]
    return np.exp2(a.ravel()).repeat(32)


def f64(x):
    return np.asarray(x).astype(np.float64)


def striped8(idx):
    return np.concatenate([v.reshape(-1, 16).T for v in idx]).astype(np.uint16)


def unstriped8(offs):
    return np.stack([offs[16 * g:16 * g + 16].T.reshape(-1) for g in range(8)]).astype(np.int64)


E2M1 = np.array([0.0, 0.5, 1.0, 1.5, 2.0, 3.0, 4.0, 6.0, -0.0, -0.5, -1.0, -1.5, -2.0, -3.0, -4.0, -6.0])


def pack_weight(w, fmt):
    k, n = w.shape
    w = f64(np.asarray(w, np.float32).astype(ml_dtypes.bfloat16)).reshape(k // 32, 32, n)
    amax = np.abs(w).max(1)
    if fmt == "e4m3":
        byte = np.frexp(amax)[1] - 1 + 127 - 7
    else:
        mant, ex = np.frexp(amax / 6.0)
        byte = np.where(mant > 0.5, ex, ex - 1) + 127
    byte = np.clip(np.where(amax > 0, byte, 1), 1, 254)
    scaled = (w * np.exp2(127.0 - byte)[:, None, :]).reshape(k, n).astype(np.float32)
    by_word = np.ascontiguousarray(scaled.reshape(k // 512, 128, 4, n).transpose(0, 1, 3, 2))
    if fmt == "e4m3":
        words = by_word.astype(ml_dtypes.float8_e4m3fn).view(np.uint8)
    else:
        c = by_word.astype(ml_dtypes.float4_e2m1fn).view(np.uint8) & 0xF
        words = (c[..., 0::2] | (c[..., 1::2] << 4)).reshape(k // 512, 128, 2 * n)
    return np.ascontiguousarray(words), np.ascontiguousarray(byte.astype(np.uint8).reshape(k // 512, 16, n))


def unpack_weight(words, scales, fmt):
    g, _, n = scales.shape
    words = np.ascontiguousarray(words).reshape(g, 128, n, -1)
    if fmt == "e4m3":
        vals = words.view(ml_dtypes.float8_e4m3fn).astype(np.float64)
    else:
        nib = np.empty((g, 128, n, 4), np.uint8)
        nib[..., 0::2] = words & 0xF
        nib[..., 1::2] = words >> 4
        vals = E2M1[nib]
    vals = vals * np.repeat(np.exp2(scales.astype(np.float64) - 127.0), 8, axis=1)[..., None]
    return vals.transpose(0, 1, 3, 2).reshape(g * 512, n)


def gelu(v):
    return 0.5 * v * (1.0 + np.tanh(np.sqrt(2.0 / np.pi) * (v + 0.044715 * v**3)))


K, M, T, S = 1024, 1024, 1024, 512


def setup_inputs():
    n = np.random.standard_normal
    s = mx_kscale(K)[:, None]
    p_w = pack_weight(n((K, M)) / np.sqrt(K) / s, "e2m1")
    return {
        "xT": (n((K, T)) * s).astype(np.float32),
        "w_words": p_w[0],
        "w_scales": p_w[1],
        "wgt": np.repeat(np.random.uniform(0.5, 2.0, (8, S)), 16, axis=0).astype(np.float32),
        "b": (0.3 * n(1024)).astype(np.float32),
        "offs": striped8(np.stack([np.random.permutation(T)[:S] for _ in range(8)])),
    }


def reference(xT, w_words, w_scales, wgt, b, offs):
    idx = unstriped8(offs)
    group = np.arange(K) % 512 // 64
    xg = f64(wgt)[np.arange(K) // 4 % 128] * f64(xT)[np.arange(K)[:, None], idx[group]]
    xT_ = mxq(xg, 0, "e4m3")
    w_ = unpack_weight(w_words, w_scales, "e2m1")
    y = w_.T @ xT_
    return gelu(y + f64(b)[:, None])

@@ -1,0 +1,160 @@
+from contextlib import ExitStack
+
+import concourse.mybir as mybir
+from concourse.masks import make_identity
+
+K, N_OUT, T, S = 1024, 1024, 1024, 512
+FLOPS = 2 * K * N_OUT * S
+
+F32 = mybir.dt.float32
+BF16 = mybir.dt.bfloat16
+I32 = mybir.dt.int32
+U32 = mybir.dt.uint32
+U16 = mybir.dt.uint16
+U8 = mybir.dt.uint8
+FP8X4 = mybir.dt.float8_e4m3fn_x4
+FP4X4 = mybir.dt.float4_e2m1fn_x4
+MULT = mybir.AluOpType.mult
+GELU = mybir.ActivationFunctionType.Gelu_apprx_tanh
+
+P = 128
+PASSES = 2
+PACK = 4
+NT = N_OUT // P
+H = S // 2
+
+
+def tile_list_heads_gelu_kernel(tc, xT, w_words, w_scales, wgt, b, offs, out):
+    nc = tc.nc
+    with ExitStack() as ctx:
+        keep = ctx.enter_context(tc.tile_pool(name="keep", bufs=1))
+        psum = ctx.enter_context(tc.psum_pool(name="psum", bufs=1))
+
+        lists = keep.tile([P, S // 16], U16, name="lists")
+        wg = keep.tile([P, S], F32, name="wg")
+        planes = [keep.tile([P, T], F32, name=f"plane{i}") for i in range(PASSES * PACK)]
+        w_sb = keep.tile([P, PASSES, 2 * N_OUT], U8, name="w_sb", align_bytes=256)
+        ws_sb = keep.tile([P, PASSES, N_OUT], U8, name="ws_sb", align_bytes=256)
+        b_rows = keep.tile([P, P], F32, name="b_rows")
+        b_cols = keep.tile([P, NT], F32, name="b_cols")
+        ident = keep.tile([P, P], F32, name="ident")
+        warm = keep.tile([P, 1], F32, name="warm")
+        picked = [keep.tile([P, PACK, S], F32, name=f"picked{a}") for a in range(PASSES)]
+        grouped = [keep.tile([P, S, PACK], BF16, name=f"grouped{a}", align_bytes=256) for a in range(PASSES)]
+        codes = [keep.tile([P, S], U32, name=f"codes{a}", align_bytes=256) for a in range(PASSES)]
+        scales = [keep.tile([P, S], U8, name=f"scales{a}", align_bytes=256) for a in range(PASSES)]
+        result = keep.tile([P, NT, S], F32, name="result")
+        acc = [psum.tile([P, S], F32, name=f"acc{t}") for t in range(NT)]
+
+        x_view = xT.rearrange("(a p i) t -> a i p t", a=PASSES, i=PACK)
+
+        def load_plane(n):
+            nc.sync.dma_start(planes[n][:], x_view[n // PACK, n % PACK])
+
+        def load_w(a):
+            nc.sync.dma_start(w_sb[:, a, :].bitcast(I32), w_words[a].bitcast(I32))
+
+        nc.sync.dma_start(lists[:], offs)
+        nc.sync.dma_start(wg[:], wgt)
+        nc.vector.memset(ws_sb[:].rearrange("p a n -> p (a n)").bitcast(I32), 0)
+        nc.vector.memset(b_rows[:], 0.0)
+        nc.vector.memset(warm[:], 0.0)
+        nc.scalar.activation(warm[:], warm[:], GELU)
+        for q in range(4):
+            nc.scalar.dma_start(
+                ws_sb[32 * q : 32 * q + 4, :, :].bitcast(I32),
+                w_scales[:, 4 * q : 4 * q + 4, :].rearrange("a q n -> q a n").bitcast(I32),
+            )
+        nc.scalar.dma_start(b_rows[0:NT, :], b.rearrange("(c p) -> c p", p=P))
+        for n in range(8):
+            load_plane(n)
+        load_w(0)
+        load_w(1)
+
+        make_identity(nc, ident[:])
+        nc.tensor.transpose(acc[NT - 1][:, 0:P], b_rows[:], ident[:])
+        nc.scalar.copy(b_cols[:], acc[NT - 1][:, 0:NT])
+
+        def gather(n, c0, cn):
+            nc.vector.tensor_tensor(
+                picked[n // PACK][:, n % PACK, c0 : c0 + cn],
+                planes[n][:].indirect(lists[:, c0 // 16 : (c0 + cn) // 16]),
+                wg[:, c0 : c0 + cn],
+                MULT,
+            )
+
+        def interleave(eng, a, c0, cn, i0=0, i1=PACK):
+            dst = grouped[a][:, c0 : c0 + cn, i0:i1].rearrange("p (c j) i -> p c i j", j=4)
+            src = picked[a][:, i0:i1, c0 : c0 + cn].rearrange("p i (c j) -> p c i j", j=4)
+            if eng == "v":
+                nc.vector.tensor_copy(dst, src)
+            else:
+                nc.scalar.copy(dst, src)
+
+        def quantize(a, c0, cn):
+            nc.vector.quantize_mx(
+                out=codes[a][:, c0 : c0 + cn].bitcast(FP8X4),
+                scales=scales[a][:, c0 : c0 + cn],
+                in_=grouped[a][:, c0 : c0 + cn, :].rearrange("p c i -> p (c i)"),
+            )
+
+        def multiply(a, t, c0, cn):
+            nc.tensor.matmul_mx(
+                out=acc[t][:, c0 : c0 + cn],
+                lhsT=w_sb[:, a, 2 * P * t : 2 * P * (t + 1)].bitcast(FP4X4),
+                lhsT_scale=ws_sb[:, a, P * t : P * (t + 1)],
+                rhs=codes[a][:, c0 : c0 + cn].bitcast(FP8X4),
+                rhs_scale=scales[a][:, c0 : c0 + cn],
+                start=(a == 0),
+                stop=(a == PASSES - 1),
+            )
+
+        out_view = out.rearrange("(t p) j -> p t j", p=P)
+
+        def finish(t, c0, cn):
+            nc.scalar.activation(result[:, t, c0 : c0 + cn], acc[t][:, c0 : c0 + cn], GELU, bias=b_cols[:, t : t + 1])
+
+        def store(t0, tn, c0, cn):
+            nc.sync.dma_start(out_view[:, t0 : t0 + tn, c0 : c0 + cn], result[:, t0 : t0 + tn, c0 : c0 + cn])
+
+        for n in range(4):
+            gather(n, 0, H)
+            gather(n, H, H)
+        interleave("s", 0, 0, H)
+        interleave("s", 0, H, H)
+        gather(4, 0, H)
+        gather(4, H, H)
+        gather(5, 0, H)
+        interleave("s", 1, 0, H, 0, 2)
+        quantize(0, 0, S)
+        gather(5, H, H)
+        interleave("s", 1, H, H, 0, 2)
+        gather(6, 0, H)
+        for t in range(NT):
+            multiply(0, t, 0, 128)
+        gather(7, 0, 128)
+        gather(7, 128, 128)
+        interleave("v", 1, 0, 128, 2, 4)
+        interleave("v", 1, 128, 128, 2, 4)
+        quantize(1, 0, 128)
+        quantize(1, 128, 128)
+        gather(6, H, H)
+        gather(7, H, H)
+        interleave("v", 1, H, H, 2, 4)
+        quantize(1, H, H)
+        for t in range(NT):
+            multiply(1, t, 0, 128)
+            multiply(0, t, 128, 128)
+            multiply(1, t, 128, 128)
+            finish(t, 0, H)
+            if t % 2 == 1:
+                store(t - 1, 2, 0, H)
+        for t in range(NT):
+            multiply(0, t, 256, 128)
+        for t in range(NT):
+            multiply(1, t, 256, 128)
+            multiply(0, t, 384, 128)
+            multiply(1, t, 384, 128)
+            finish(t, H, H)
+            if t % 2 == 1:
+                store(t - 1, 2, H, H)

@@ -54,20 +54,22 @@ def tile_list_heads_gelu_kernel(tc, xT, w_words, w_scales, wgt, b, offs, out):
         def load_w(a):
             nc.sync.dma_start(w_sb[:, a, :].bitcast(I32), w_words[a].bitcast(I32))
 
-        nc.sync.dma_start(lists[:], offs)
-        nc.sync.dma_start(wg[:], wgt)
-        nc.vector.memset(ws_sb[:].rearrange("p a n -> p (a n)").bitcast(I32), 0)
         nc.vector.memset(b_rows[:], 0.0)
         nc.vector.memset(warm[:], 0.0)
+        nc.vector.memset(ws_sb[:].rearrange("p a n -> p (a n)").bitcast(I32), 0)
+        nc.scalar.dma_start(b_rows[0:NT, :], b.rearrange("(c p) -> c p", p=P))
         nc.scalar.activation(warm[:], warm[:], GELU)
+        nc.sync.dma_start(lists[:], offs)
+        load_plane(0)
+        nc.sync.dma_start(wg[:, 0:H], wgt[:, 0:H])
+        nc.sync.dma_start(wg[:, H:S], wgt[:, H:S])
+        for n in range(1, 8):
+            load_plane(n)
         for q in range(4):
-            nc.scalar.dma_start(
+            nc.sync.dma_start(
                 ws_sb[32 * q : 32 * q + 4, :, :].bitcast(I32),
                 w_scales[:, 4 * q : 4 * q + 4, :].rearrange("a q n -> q a n").bitcast(I32),
             )
-        nc.scalar.dma_start(b_rows[0:NT, :], b.rearrange("(c p) -> c p", p=P))
-        for n in range(8):
-            load_plane(n)
         load_w(0)
         load_w(1)
 
@@ -126,7 +128,7 @@ def tile_list_heads_gelu_kernel(tc, xT, w_words, w_scales, wgt, b, offs, out):
         gather(4, H, H)
         gather(5, 0, H)
         interleave("s", 1, 0, H, 0, 2)
-        quantize(0, 0, S)
+        quantize(0, 0, H)
         gather(5, H, H)
         interleave("s", 1, H, H, 0, 2)
         gather(6, 0, H)
@@ -140,8 +142,11 @@ def tile_list_heads_gelu_kernel(tc, xT, w_words, w_scales, wgt, b, offs, out):
         quantize(1, 128, 128)
         gather(6, H, H)
         gather(7, H, H)
-        interleave("v", 1, H, H, 2, 4)
-        quantize(1, H, H)
+        quantize(0, H, H)
+        interleave("v", 1, 256, 128, 2, 4)
+        interleave("v", 1, 384, 128, 2, 4)
+        quantize(1, 256, 128)
+        quantize(1, 384, 128)
         for t in range(NT):
             multiply(1, t, 0, 128)
             multiply(0, t, 128, 128)
@@ -156,5 +161,7 @@ def tile_list_heads_gelu_kernel(tc, xT, w_words, w_scales, wgt, b, offs, out):
             multiply(0, t, 384, 128)
             multiply(1, t, 384, 128)
             finish(t, H, H)
-            if t % 2 == 1:
+            if t in (1, 3, 5):
                 store(t - 1, 2, H, H)
+            elif t > 5:
+                store(t, 1, H, H)

@@ -22,6 +22,7 @@ PASSES = 2
 PACK = 4
 NT = N_OUT // P
 H = S // 2
+SPLIT = 4
 
 
 def tile_list_heads_gelu_kernel(tc, xT, w_words, w_scales, wgt, b, offs, out):
@@ -51,8 +52,17 @@ def tile_list_heads_gelu_kernel(tc, xT, w_words, w_scales, wgt, b, offs, out):
         def load_plane(n):
             nc.sync.dma_start(planes[n][:], x_view[n // PACK, n % PACK])
 
-        def load_w(a):
-            nc.sync.dma_start(w_sb[:, a, :].bitcast(I32), w_words[a].bitcast(I32))
+        def load_w_scales(a):
+            for q in range(4):
+                nc.sync.dma_start(
+                    ws_sb[32 * q : 32 * q + 4, a, :].bitcast(I32), w_scales[a, 4 * q : 4 * q + 4, :].bitcast(I32)
+                )
+
+        w_view = w_words.rearrange("a p n -> p a n")
+
+        def load_w(a0, a1, t0, t1):
+            cols = slice(2 * P * t0, 2 * P * t1)
+            nc.sync.dma_start(w_sb[:, a0:a1, cols].bitcast(I32), w_view[:, a0:a1, cols].bitcast(I32))
 
         nc.vector.memset(b_rows[:], 0.0)
         nc.vector.memset(warm[:], 0.0)
@@ -63,15 +73,16 @@ def tile_list_heads_gelu_kernel(tc, xT, w_words, w_scales, wgt, b, offs, out):
         load_plane(0)
         nc.sync.dma_start(wg[:, 0:H], wgt[:, 0:H])
         nc.sync.dma_start(wg[:, H:S], wgt[:, H:S])
-        for n in range(1, 8):
+        for n in range(1, 6):
             load_plane(n)
-        for q in range(4):
-            nc.sync.dma_start(
-                ws_sb[32 * q : 32 * q + 4, :, :].bitcast(I32),
-                w_scales[:, 4 * q : 4 * q + 4, :].rearrange("a q n -> q a n").bitcast(I32),
-            )
-        load_w(0)
-        load_w(1)
+        load_w_scales(0)
+        load_w(0, 1, SPLIT, NT)
+        for n in range(6, 8):
+            load_plane(n)
+        load_w(0, 1, 0, SPLIT)
+        load_w_scales(1)
+        load_w(1, 2, 0, SPLIT)
+        load_w(1, 2, SPLIT, NT)
 
         make_identity(nc, ident[:])
         nc.tensor.transpose(acc[NT - 1][:, 0:P], b_rows[:], ident[:])
@@ -128,40 +139,50 @@ def tile_list_heads_gelu_kernel(tc, xT, w_words, w_scales, wgt, b, offs, out):
         gather(4, H, H)
         gather(5, 0, H)
         interleave("s", 1, 0, H, 0, 2)
-        quantize(0, 0, H)
         gather(5, H, H)
         interleave("s", 1, H, H, 0, 2)
+        quantize(0, 0, S)
         gather(6, 0, H)
-        for t in range(NT):
-            multiply(0, t, 0, 128)
-        gather(7, 0, 128)
-        gather(7, 128, 128)
-        interleave("v", 1, 0, 128, 2, 4)
-        interleave("v", 1, 128, 128, 2, 4)
-        quantize(1, 0, 128)
-        quantize(1, 128, 128)
         gather(6, H, H)
-        gather(7, H, H)
-        quantize(0, H, H)
-        interleave("v", 1, 256, 128, 2, 4)
-        interleave("v", 1, 384, 128, 2, 4)
-        quantize(1, 256, 128)
-        quantize(1, 384, 128)
-        for t in range(NT):
+        whole = range(SPLIT, NT)
+        halved = range(SPLIT)
+        for t in whole:
+            multiply(0, t, 0, S)
+        for q in range(2):
+            gather(7, 128 * q, 128)
+        for q in range(2):
+            interleave("v", 1, 128 * q, 128, 2, 4)
+        for q in range(2):
+            quantize(1, 128 * q, 128)
+        for q in range(2, 4):
+            gather(7, 128 * q, 128)
+        for q in range(2, 4):
+            interleave("v", 1, 128 * q, 128, 2, 4)
+        for q in range(2, 4):
+            quantize(1, 128 * q, 128)
+        for t in halved:
+            multiply(0, t, 0, 128)
+        for t in halved:
             multiply(1, t, 0, 128)
             multiply(0, t, 128, 128)
             multiply(1, t, 128, 128)
             finish(t, 0, H)
-            if t % 2 == 1:
+            if t < 2:
+                store(t, 1, 0, H)
+            elif t == 3:
                 store(t - 1, 2, 0, H)
-        for t in range(NT):
-            multiply(0, t, 256, 128)
-        for t in range(NT):
-            multiply(1, t, 256, 128)
-            multiply(0, t, 384, 128)
-            multiply(1, t, 384, 128)
+        for t in whole:
+            multiply(1, t, 0, S)
+            finish(t, 0, S)
+            store(t, 1, 0, S)
+        for t in halved:
+            for q in range(2, 4):
+                multiply(0, t, 128 * q, 128)
+                multiply(1, t, 128 * q, 128)
             finish(t, H, H)
-            if t in (1, 3, 5):
+            if t == 1:
                 store(t - 1, 2, H, H)
-            elif t > 5:
+            elif t == 2:
                 store(t, 1, H, H)
+            elif t == 3:
+                nc.scalar.dma_start(out_view[:, t, H:S], result[:, t, H:S])

from contextlib import ExitStack

import concourse.mybir as mybir
from concourse.masks import make_identity

K, N_OUT, T, S = 1024, 1024, 1024, 512
FLOPS = 2 * K * N_OUT * S

F32 = mybir.dt.float32
BF16 = mybir.dt.bfloat16
I32 = mybir.dt.int32
U32 = mybir.dt.uint32
U16 = mybir.dt.uint16
U8 = mybir.dt.uint8
FP8X4 = mybir.dt.float8_e4m3fn_x4
FP4X4 = mybir.dt.float4_e2m1fn_x4
MULT = mybir.AluOpType.mult
GELU = mybir.ActivationFunctionType.Gelu_apprx_tanh

P = 128
PASSES = 2
PACK = 4
NT = N_OUT // P
H = S // 2
SPLIT = 4


def tile_list_heads_gelu_kernel(tc, xT, w_words, w_scales, wgt, b, offs, out):
    nc = tc.nc
    with ExitStack() as ctx:
        keep = ctx.enter_context(tc.tile_pool(name="keep", bufs=1))
        psum = ctx.enter_context(tc.psum_pool(name="psum", bufs=1))

        lists = keep.tile([P, S // 16], U16, name="lists")
        wg = keep.tile([P, S], F32, name="wg")
        planes = [keep.tile([P, T], F32, name=f"plane{i}") for i in range(PASSES * PACK)]
        w_sb = keep.tile([P, PASSES, 2 * N_OUT], U8, name="w_sb", align_bytes=256)
        ws_sb = keep.tile([P, PASSES, N_OUT], U8, name="ws_sb", align_bytes=256)
        b_rows = keep.tile([P, P], F32, name="b_rows")
        b_cols = keep.tile([P, NT], F32, name="b_cols")
        ident = keep.tile([P, P], F32, name="ident")
        warm = keep.tile([P, 1], F32, name="warm")
        picked = [keep.tile([P, PACK, S], F32, name=f"picked{a}") for a in range(PASSES)]
        grouped = [keep.tile([P, S, PACK], BF16, name=f"grouped{a}", align_bytes=256) for a in range(PASSES)]
        codes = [keep.tile([P, S], U32, name=f"codes{a}", align_bytes=256) for a in range(PASSES)]
        scales = [keep.tile([P, S], U8, name=f"scales{a}", align_bytes=256) for a in range(PASSES)]
        result = keep.tile([P, NT, S], F32, name="result")
        acc = [psum.tile([P, S], F32, name=f"acc{t}") for t in range(NT)]

        x_view = xT.rearrange("(a p i) t -> a i p t", a=PASSES, i=PACK)

        def load_plane(n):
            nc.sync.dma_start(planes[n][:], x_view[n // PACK, n % PACK])

        def load_w_scales(a):
            for q in range(4):
                nc.sync.dma_start(
                    ws_sb[32 * q : 32 * q + 4, a, :].bitcast(I32), w_scales[a, 4 * q : 4 * q + 4, :].bitcast(I32)
                )

        w_view = w_words.rearrange("a p n -> p a n")

        def load_w(a0, a1, t0, t1):
            cols = slice(2 * P * t0, 2 * P * t1)
            nc.sync.dma_start(w_sb[:, a0:a1, cols].bitcast(I32), w_view[:, a0:a1, cols].bitcast(I32))

        nc.vector.memset(b_rows[:], 0.0)
        nc.vector.memset(warm[:], 0.0)
        nc.vector.memset(ws_sb[:].rearrange("p a n -> p (a n)").bitcast(I32), 0)
        nc.scalar.dma_start(b_rows[0:NT, :], b.rearrange("(c p) -> c p", p=P))
        nc.scalar.activation(warm[:], warm[:], GELU)
        nc.sync.dma_start(lists[:], offs)
        load_plane(0)
        nc.sync.dma_start(wg[:, 0:H], wgt[:, 0:H])
        nc.sync.dma_start(wg[:, H:S], wgt[:, H:S])
        for n in range(1, 6):
            load_plane(n)
        load_w_scales(0)
        load_w(0, 1, SPLIT, NT)
        for n in range(6, 8):
            load_plane(n)
        load_w(0, 1, 0, SPLIT)
        load_w_scales(1)
        load_w(1, 2, 0, SPLIT)
        load_w(1, 2, SPLIT, NT)

        make_identity(nc, ident[:])
        nc.tensor.transpose(acc[NT - 1][:, 0:P], b_rows[:], ident[:])
        nc.scalar.copy(b_cols[:], acc[NT - 1][:, 0:NT])

        def gather(n, c0, cn):
            nc.vector.tensor_tensor(
                picked[n // PACK][:, n % PACK, c0 : c0 + cn],
                planes[n][:].indirect(lists[:, c0 // 16 : (c0 + cn) // 16]),
                wg[:, c0 : c0 + cn],
                MULT,
            )

        def interleave(eng, a, c0, cn, i0=0, i1=PACK):
            dst = grouped[a][:, c0 : c0 + cn, i0:i1].rearrange("p (c j) i -> p c i j", j=4)
            src = picked[a][:, i0:i1, c0 : c0 + cn].rearrange("p i (c j) -> p c i j", j=4)
            if eng == "v":
                nc.vector.tensor_copy(dst, src)
            else:
                nc.scalar.copy(dst, src)

        def quantize(a, c0, cn):
            nc.vector.quantize_mx(
                out=codes[a][:, c0 : c0 + cn].bitcast(FP8X4),
                scales=scales[a][:, c0 : c0 + cn],
                in_=grouped[a][:, c0 : c0 + cn, :].rearrange("p c i -> p (c i)"),
            )

        def multiply(a, t, c0, cn):
            nc.tensor.matmul_mx(
                out=acc[t][:, c0 : c0 + cn],
                lhsT=w_sb[:, a, 2 * P * t : 2 * P * (t + 1)].bitcast(FP4X4),
                lhsT_scale=ws_sb[:, a, P * t : P * (t + 1)],
                rhs=codes[a][:, c0 : c0 + cn].bitcast(FP8X4),
                rhs_scale=scales[a][:, c0 : c0 + cn],
                start=(a == 0),
                stop=(a == PASSES - 1),
            )

        out_view = out.rearrange("(t p) j -> p t j", p=P)

        def finish(t, c0, cn):
            nc.scalar.activation(result[:, t, c0 : c0 + cn], acc[t][:, c0 : c0 + cn], GELU, bias=b_cols[:, t : t + 1])

        def store(t0, tn, c0, cn):
            nc.sync.dma_start(out_view[:, t0 : t0 + tn, c0 : c0 + cn], result[:, t0 : t0 + tn, c0 : c0 + cn])

        for n in range(4):
            gather(n, 0, H)
            gather(n, H, H)
        interleave("s", 0, 0, H)
        interleave("s", 0, H, H)
        gather(4, 0, H)
        gather(4, H, H)
        gather(5, 0, H)
        interleave("s", 1, 0, H, 0, 2)
        gather(5, H, H)
        interleave("s", 1, H, H, 0, 2)
        quantize(0, 0, S)
        gather(6, 0, H)
        gather(6, H, H)
        whole = range(SPLIT, NT)
        halved = range(SPLIT)
        for t in whole:
            multiply(0, t, 0, S)
        for q in range(2):
            gather(7, 128 * q, 128)
        for q in range(2):
            interleave("v", 1, 128 * q, 128, 2, 4)
        for q in range(2):
            quantize(1, 128 * q, 128)
        for q in range(2, 4):
            gather(7, 128 * q, 128)
        for q in range(2, 4):
            interleave("v", 1, 128 * q, 128, 2, 4)
        for q in range(2, 4):
            quantize(1, 128 * q, 128)
        for t in halved:
            multiply(0, t, 0, 128)
        for t in halved:
            multiply(1, t, 0, 128)
            multiply(0, t, 128, 128)
            multiply(1, t, 128, 128)
            finish(t, 0, H)
            if t < 2:
                store(t, 1, 0, H)
            elif t == 3:
                store(t - 1, 2, 0, H)
        for t in whole:
            multiply(1, t, 0, S)
            finish(t, 0, S)
            store(t, 1, 0, S)
        for t in halved:
            for q in range(2, 4):
                multiply(0, t, 128 * q, 128)
                multiply(1, t, 128 * q, 128)
            finish(t, H, H)
            if t == 1:
                store(t - 1, 2, H, H)
            elif t == 2:
                store(t, 1, H, H)
            elif t == 3:
                nc.scalar.dma_start(out_view[:, t, H:S], result[:, t, H:S])
